import numpy as np
import ml_dtypes


def mxq(x, axis, fmt="e4m3"):
    dtype, down = {"e4m3": (ml_dtypes.float8_e4m3fn, 7), "e5m2": (ml_dtypes.float8_e5m2, 14)}[fmt]
    v = np.moveaxis(np.asarray(x, np.float32).astype(ml_dtypes.bfloat16).astype(np.float64), axis, -1)
    blocks = v.reshape(v.shape[:-1] + (-1, 32))
    amax = np.abs(blocks).max(-1, keepdims=True)
    byte = np.maximum(np.where(amax > 0, np.frexp(amax)[1] - 1 + 127, 0) - down, 1)
    scale = np.exp2(byte - 127.0)
    codes = (blocks / scale).astype(np.float32).astype(dtype).astype(np.float64)
    return np.moveaxis((codes * scale).reshape(v.shape), -1, axis)


WIDE = False


def mx_kscale(k):
    if not WIDE:
        return np.ones(k)
    levels = np.array([10, -10, 5, -5, 0])
    if k % 512:
        return np.exp2(np.random.permutation(np.resize(levels, k // 32))).repeat(32)
    a = np.empty((k // 512, 16))
    for p in range(k // 512):
        a[p, :8] = np.random.permutation(np.resize(levels, 8))
        for g in range(8):
            far = levels[np.abs(levels - a[p, g]) >= 10]
            a[p, g + 8] = far[np.random.randint(len(far))]
    return np.exp2(a.ravel()).repeat(32)


def f64(x):
    return np.asarray(x).astype(np.float64)


def striped(idx):
    return np.tile(idx.reshape(-1, 16).T, (8, 1)).astype(np.uint16)


def unstriped(offs):
    return offs[:16].T.reshape(-1).astype(np.int64)


E2M1 = np.array([0.0, 0.5, 1.0, 1.5, 2.0, 3.0, 4.0, 6.0, -0.0, -0.5, -1.0, -1.5, -2.0, -3.0, -4.0, -6.0])


def pack_weight(w, fmt):
    k, n = w.shape
    w = f64(np.asarray(w, np.float32).astype(ml_dtypes.bfloat16)).reshape(k // 32, 32, n)
    amax = np.abs(w).max(1)
    if fmt == "e4m3":
        byte = np.frexp(amax)[1] - 1 + 127 - 7
    else:
        mant, ex = np.frexp(amax / 6.0)
        byte = np.where(mant > 0.5, ex, ex - 1) + 127
    byte = np.clip(np.where(amax > 0, byte, 1), 1, 254)
    scaled = (w * np.exp2(127.0 - byte)[:, None, :]).reshape(k, n).astype(np.float32)
    by_word = np.ascontiguousarray(scaled.reshape(k // 512, 128, 4, n).transpose(0, 1, 3, 2))
    if fmt == "e4m3":
        words = by_word.astype(ml_dtypes.float8_e4m3fn).view(np.uint8)
    else:
        c = by_word.astype(ml_dtypes.float4_e2m1fn).view(np.uint8) & 0xF
        words = (c[..., 0::2] | (c[..., 1::2] << 4)).reshape(k // 512, 128, 2 * n)
    return np.ascontiguousarray(words), np.ascontiguousarray(byte.astype(np.uint8).reshape(k // 512, 16, n))


def unpack_weight(words, scales, fmt):
    g, _, n = scales.shape
    words = np.ascontiguousarray(words).reshape(g, 128, n, -1)
    if fmt == "e4m3":
        vals = words.view(ml_dtypes.float8_e4m3fn).astype(np.float64)
    else:
        nib = np.empty((g, 128, n, 4), np.uint8)
        nib[..., 0::2] = words & 0xF
        nib[..., 1::2] = words >> 4
        vals = E2M1[nib]
    vals = vals * np.repeat(np.exp2(scales.astype(np.float64) - 127.0), 8, axis=1)[..., None]
    return vals.transpose(0, 1, 3, 2).reshape(g * 512, n)


def silu(v):
    return v / (1.0 + np.exp(-np.maximum(v, -700.0)))


K, T, E, C, H, N = 512, 1536, 8, 128, 512, 128


def by_expert(wq, xq):
    return np.concatenate([wq[e].T @ xq[:, e * C:(e + 1) * C] for e in range(E)], axis=1)


def setup_inputs():
    n = np.random.standard_normal
    s = mx_kscale(K)[:, None]
    u = mx_kscale(H)
    w1 = [pack_weight(m, "e2m1") for m in n((E, K, H)) / np.sqrt(K) / s[None]]
    w3 = [pack_weight(m, "e2m1") for m in n((E, K, H)) / np.sqrt(K) / s[None] * u[None, None, :]]
    w2 = [pack_weight(m, "e2m1") for m in n((E, H, N)) / np.sqrt(H) / u[None, :, None]]
    return {
        "xT": (n((K, T)) * s).astype(np.float32),
        "xr": n((N, T)).astype(np.float32),
        "w1_words": np.stack([m[0] for m in w1]),
        "w1_scales": np.stack([m[1] for m in w1]),
        "w3_words": np.stack([m[0] for m in w3]),
        "w3_scales": np.stack([m[1] for m in w3]),
        "w2_words": np.stack([m[0] for m in w2]),
        "w2_scales": np.stack([m[1] for m in w2]),
        "gate": np.tile(np.random.uniform(0.2, 1.0, E * C), (N, 1)).astype(np.float32),
        "offs": striped(np.random.permutation(T)[:E * C]),
    }


def reference(xT, xr, w1_words, w1_scales, w3_words, w3_scales, w2_words, w2_scales, gate, offs):
    idx = unstriped(offs)
    w1 = np.stack([unpack_weight(w1_words[e], w1_scales[e], "e2m1") for e in range(E)])
    w3 = np.stack([unpack_weight(w3_words[e], w3_scales[e], "e2m1") for e in range(E)])
    w2 = np.stack([unpack_weight(w2_words[e], w2_scales[e], "e2m1") for e in range(E)])
    xq = mxq(f64(xT)[:, idx], 0, "e4m3")
    h = silu(by_expert(w1, xq))
    h = h * by_expert(w3, xq)
    y = by_expert(w2, mxq(h, 0, "e4m3"))
    out = f64(xr).copy()
    out[:, idx] += f64(gate) * y
    return out

@@ -1,0 +1,210 @@
+from contextlib import ExitStack
+
+import concourse.mybir as mybir
+from concourse.masks import make_identity
+
+K, T, E, C, H, N = 512, 1536, 8, 128, 512, 128
+S = E * C
+FLOPS = 2 * S * (2 * K * H + H * N)
+
+P = 128
+PACK = 4
+F32 = mybir.dt.float32
+BF16 = mybir.dt.bfloat16
+I32 = mybir.dt.int32
+U32 = mybir.dt.uint32
+U16 = mybir.dt.uint16
+U8 = mybir.dt.uint8
+FP8X4 = mybir.dt.float8_e4m3fn_x4
+FP4X4 = mybir.dt.float4_e2m1fn_x4
+MULT = mybir.AluOpType.mult
+ADD = mybir.AluOpType.add
+COPY = mybir.ActivationFunctionType.Copy
+SILU = mybir.ActivationFunctionType.Silu
+
+CHUNKS = ((0, 512), (512, 512), (1024, 256), (1280, 256))
+PAIR = 2 * C
+PAIRS = E // 2
+OUT_CUTS = ((0, 640), (640, 512), (1152, 384))
+
+
+def tile_moe_res_glu_silu_kernel(tc, xT, xr, w1_words, w1_scales, w3_words, w3_scales, w2_words, w2_scales, gate, offs, out):
+    nc = tc.nc
+    with ExitStack() as ctx:
+        keep = ctx.enter_context(tc.tile_pool(name="keep", bufs=1))
+        ring = ctx.enter_context(tc.tile_pool(name="ring", bufs=4))
+        psum = ctx.enter_context(tc.psum_pool(name="psum", bufs=2))
+
+        offsets = keep.tile([P, S // 16], U16, name="offsets")
+        ident = keep.tile([P, P], F32, name="ident", align_bytes=64)
+        warm = keep.tile([P, 1], F32, name="warm")
+        warm_out = keep.tile([P, 1], F32, name="warm_out")
+        x_codes = keep.tile([P, T], U32, name="x_codes", align_bytes=64)
+        x_scales = keep.tile([P, T], U8, name="x_scales", align_bytes=64)
+        s1 = keep.tile([P, E, H], U8, name="s1", align_bytes=64)
+        s3 = keep.tile([P, E, H], U8, name="s3", align_bytes=64)
+        s2 = keep.tile([P, E, N], U8, name="s2", align_bytes=64)
+        w2 = keep.tile([P, E, 2 * N], U8, name="w2", align_bytes=64)
+        gates = keep.tile([P, S], F32, name="gates", align_bytes=64)
+        resid = keep.tile([P, T], F32, name="resid", align_bytes=64)
+        back = keep.tile([P, T], F32, name="back", align_bytes=64)
+
+        nc.vector.memset(warm[:], 0.0)
+        nc.scalar.activation(warm_out[:], warm[:], SILU)
+        nc.vector.memset(s1[:].rearrange("p e i -> p (e i)").bitcast(I32), 0)
+        nc.vector.memset(s3[:].rearrange("p e i -> p (e i)").bitcast(I32), 0)
+        nc.gpsimd.memset(x_scales[:], 0)
+        nc.gpsimd.memset(s2[:].rearrange("p e i -> p (e i)").bitcast(I32), 0)
+        make_identity(nc, ident[:])
+        nc.gpsimd.memset(back[:], 0.0)
+
+        raws = []
+        for c, (c0, n) in enumerate(CHUNKS):
+            raw = keep.tile([P, PACK, n], F32, name="raw%d" % c, align_bytes=64)
+            nc.sync.dma_start(raw[:], xT[:, c0 : c0 + n].rearrange("(p j) w -> p j w", j=PACK))
+            raws.append(raw)
+        nc.sync.dma_start(offsets[:], offs)
+
+        def load_scales(tile, scales, e0, e1):
+            for q in range(4):
+                nc.sync.dma_start(
+                    tile[32 * q : 32 * q + 4, e0:e1, :].bitcast(I32),
+                    scales[e0:e1, 0, 4 * q : 4 * q + 4, :].bitcast(I32).rearrange("e q i -> q e i"),
+                )
+
+        w1, w3 = [], []
+
+        def load_words(pair):
+            for held, words, label in ((w1, w1_words, "w1"), (w3, w3_words, "w3")):
+                tile = keep.tile([P, 2, 2 * H], U8, name="%s_%d" % (label, pair), align_bytes=64)
+                nc.sync.dma_start(
+                    tile[:].bitcast(I32),
+                    words[2 * pair : 2 * pair + 2, 0].bitcast(I32).rearrange("e p b -> p e b"),
+                )
+                held.append(tile)
+
+        load_scales(s1, w1_scales, 0, 2)
+        load_scales(s3, w3_scales, 0, 2)
+        load_words(0)
+        load_scales(s2, w2_scales, 0, E)
+        nc.sync.dma_start(w2[:].bitcast(I32), w2_words[:, 0].bitcast(I32).rearrange("e p b -> p e b"))
+        load_scales(s1, w1_scales, 2, E)
+        load_scales(s3, w3_scales, 2, E)
+        load_words(1)
+        nc.sync.dma_start(gates[:], gate)
+        load_words(2)
+        load_words(3)
+        nc.sync.dma_start(resid[:], xr)
+
+        for c, (c0, n) in enumerate(CHUNKS):
+            grouped = keep.tile([P, n, PACK], BF16, name="grouped%d" % c, align_bytes=64)
+            cut = n * 11 // 16
+            src = raws[c][:].rearrange("p j w -> p w j")
+            nc.vector.tensor_copy(grouped[:, 0:cut, :], src[:, 0:cut, :])
+            nc.scalar.activation(grouped[:, cut:n, :], src[:, cut:n, :], COPY)
+            nc.vector.quantize_mx(
+                out=x_codes[:, c0 : c0 + n].bitcast(FP8X4),
+                scales=x_scales[:, c0 : c0 + n],
+                in_=grouped[:].rearrange("p w j -> p (w j)"),
+            )
+
+        picked = []
+
+        def gather(pair):
+            where = offsets[:, pair * (PAIR // 16) : (pair + 1) * (PAIR // 16)]
+            codes = keep.tile([P, PAIR], U32, name="codes%d" % pair, align_bytes=64)
+            scales = keep.tile([P, PAIR], U8, name="scales%d" % pair, align_bytes=64)
+            nc.vector.tensor_copy(codes[:], x_codes[:].indirect(where))
+            nc.vector.tensor_copy(scales[:], x_scales[:].indirect(where))
+            picked.append((codes, scales))
+
+        def first(e):
+            codes, scales = picked[e // 2]
+            cols = slice(e % 2 * C, (e % 2 + 1) * C)
+            sums = []
+            for held, plane, label in ((w1, s1, "a1"), (w3, s3, "a3")):
+                acc = psum.tile([P, H], F32, name=label)
+                nc.tensor.matmul_mx(
+                    out=acc[:],
+                    lhsT=codes[:, cols].bitcast(FP8X4),
+                    lhsT_scale=scales[:, cols],
+                    rhs=held[e // 2][:, e % 2, :].bitcast(FP4X4),
+                    rhs_scale=plane[:, e, :],
+                    start=True,
+                    stop=True,
+                )
+                sums.append(acc)
+            act = ring.tile([P, H], F32, name="act")
+            nc.scalar.activation(act[:], sums[0][:], SILU)
+            return sums[1], act
+
+        def product(a3, act):
+            h = ring.tile([P, H], BF16, name="h", align_bytes=64)
+            nc.vector.tensor_tensor(h[:], a3[:], act[:], MULT)
+            turned = psum.tile([P, 2, C], F32, name="turned")
+            words = h[:].bitcast(F32)
+            for u in range(2):
+                nc.tensor.transpose(turned[:, u, :], words[:, u : H // 2 : 2], ident[:])
+            h_grouped = ring.tile([P, C * PACK], BF16, name="h_grouped", align_bytes=64)
+            nc.scalar.copy(
+                h_grouped[:].bitcast(F32).rearrange("p (r u) -> p r u", u=2),
+                turned[:].rearrange("p u r -> p r u"),
+            )
+            return h_grouped
+
+        def second(e, h_grouped, y):
+            h_codes = ring.tile([P, C], U32, name="h_codes", align_bytes=64)
+            h_scales = ring.tile([P, C], U8, name="h_scales", align_bytes=64)
+            nc.vector.quantize_mx(out=h_codes[:].bitcast(FP8X4), scales=h_scales[:], in_=h_grouped[:])
+            nc.tensor.matmul_mx(
+                out=y[:, e % 2, :],
+                lhsT=w2[:, e, :].bitcast(FP4X4),
+                lhsT_scale=s2[:, e, :],
+                rhs=h_codes[:].bitcast(FP8X4),
+                rhs_scale=h_scales[:],
+                start=True,
+                stop=True,
+            )
+
+        def scatter(pair, gated):
+            where = offsets[:, pair * (PAIR // 16) : (pair + 1) * (PAIR // 16)]
+            nc.vector.tensor_copy(back[:].indirect(where), gated[:])
+
+        sums = {}
+        gated = {}
+
+        def weigh(pair, y):
+            tile = ring.tile([P, PAIR], F32, name="gated")
+            nc.vector.tensor_tensor(
+                tile[:], y[:].rearrange("p b c -> p (b c)"), gates[:, pair * PAIR : (pair + 1) * PAIR], MULT
+            )
+            gated[pair] = tile
+
+        gather(0)
+        sums[0] = first(0)
+        sums[1] = first(1)
+        gather(1)
+        y = None
+        for pair in range(PAIRS):
+            grouped = []
+            for b in range(2):
+                grouped.append(product(*sums[2 * pair + b]))
+                if pair + 1 < PAIRS:
+                    sums[2 * pair + 2 + b] = first(2 * pair + 2 + b)
+            if pair >= 1:
+                weigh(pair - 1, y)
+            if pair + 2 < PAIRS:
+                gather(pair + 2)
+            if pair >= 2:
+                scatter(pair - 2, gated[pair - 2])
+            y = psum.tile([P, 2, C], F32, name="y")
+            for b in range(2):
+                second(2 * pair + b, grouped[b], y)
+        scatter(PAIRS - 2, gated[PAIRS - 2])
+        weigh(PAIRS - 1, y)
+        scatter(PAIRS - 1, gated[PAIRS - 1])
+
+        for i, (c0, n) in enumerate(OUT_CUTS):
+            done = keep.tile([P, n], F32, name="done%d" % i, align_bytes=64)
+            nc.vector.tensor_tensor(done[:], back[:, c0 : c0 + n], resid[:, c0 : c0 + n], ADD)
+            nc.sync.dma_start(out[:, c0 : c0 + n], done[:])

@@ -32,8 +32,12 @@ def tile_moe_res_glu_silu_kernel(tc, xT, xr, w1_words, w1_scales, w3_words, w3_s
     nc = tc.nc
     with ExitStack() as ctx:
         keep = ctx.enter_context(tc.tile_pool(name="keep", bufs=1))
+        three = ctx.enter_context(tc.tile_pool(name="three", bufs=3))
+        two = ctx.enter_context(tc.tile_pool(name="two", bufs=2))
         ring = ctx.enter_context(tc.tile_pool(name="ring", bufs=4))
-        psum = ctx.enter_context(tc.psum_pool(name="psum", bufs=2))
+        psum1 = ctx.enter_context(tc.psum_pool(name="psum1", bufs=1))
+        psum2 = ctx.enter_context(tc.psum_pool(name="psum2", bufs=2))
+        psum3 = ctx.enter_context(tc.psum_pool(name="psum3", bufs=3))
 
         offsets = keep.tile([P, S // 16], U16, name="offsets")
         ident = keep.tile([P, P], F32, name="ident", align_bytes=64)
@@ -42,21 +46,23 @@ def tile_moe_res_glu_silu_kernel(tc, xT, xr, w1_words, w1_scales, w3_words, w3_s
         x_codes = keep.tile([P, T], U32, name="x_codes", align_bytes=64)
         x_scales = keep.tile([P, T], U8, name="x_scales", align_bytes=64)
         s1 = keep.tile([P, E, H], U8, name="s1", align_bytes=64)
-        s3 = keep.tile([P, E, H], U8, name="s3", align_bytes=64)
+        s3 = [keep.tile([P, n, H], U8, name="s3_%d" % n, align_bytes=64) for n in (2, E - 2)]
         s2 = keep.tile([P, E, N], U8, name="s2", align_bytes=64)
         w2 = keep.tile([P, E, 2 * N], U8, name="w2", align_bytes=64)
         gates = keep.tile([P, S], F32, name="gates", align_bytes=64)
         resid = keep.tile([P, T], F32, name="resid", align_bytes=64)
         back = keep.tile([P, T], F32, name="back", align_bytes=64)
 
+        def zero_plane(engine, plane):
+            engine.memset(plane[:].rearrange("p e i -> p (e i)").bitcast(I32), 0)
+
+        zero_plane(nc.vector, s3[0])
         nc.vector.memset(warm[:], 0.0)
         nc.scalar.activation(warm_out[:], warm[:], SILU)
-        nc.vector.memset(s1[:].rearrange("p e i -> p (e i)").bitcast(I32), 0)
-        nc.vector.memset(s3[:].rearrange("p e i -> p (e i)").bitcast(I32), 0)
-        nc.gpsimd.memset(x_scales[:], 0)
-        nc.gpsimd.memset(s2[:].rearrange("p e i -> p (e i)").bitcast(I32), 0)
-        make_identity(nc, ident[:])
-        nc.gpsimd.memset(back[:], 0.0)
+        zero_plane(nc.vector, s1)
+        zero_plane(nc.vector, s3[1])
+        nc.vector.memset(back[:], 0.0)
+        nc.gpsimd.memset(x_scales[:].bitcast(I32), 0)
 
         raws = []
         for c, (c0, n) in enumerate(CHUNKS):
@@ -65,10 +71,10 @@ def tile_moe_res_glu_silu_kernel(tc, xT, xr, w1_words, w1_scales, w3_words, w3_s
             raws.append(raw)
         nc.sync.dma_start(offsets[:], offs)
 
-        def load_scales(tile, scales, e0, e1):
+        def load_scales(queue, tile, scales, e0, e1):
             for q in range(4):
-                nc.sync.dma_start(
-                    tile[32 * q : 32 * q + 4, e0:e1, :].bitcast(I32),
+                queue.dma_start(
+                    tile[32 * q : 32 * q + 4].bitcast(I32),
                     scales[e0:e1, 0, 4 * q : 4 * q + 4, :].bitcast(I32).rearrange("e q i -> q e i"),
                 )
 
@@ -83,14 +89,15 @@ def tile_moe_res_glu_silu_kernel(tc, xT, xr, w1_words, w1_scales, w3_words, w3_s
                 )
                 held.append(tile)
 
-        load_scales(s1, w1_scales, 0, 2)
-        load_scales(s3, w3_scales, 0, 2)
+        load_scales(nc.sync, s1, w1_scales, 0, E)
+        load_scales(nc.gpsimd, s3[0], w3_scales, 0, 2)
         load_words(0)
-        load_scales(s2, w2_scales, 0, E)
-        nc.sync.dma_start(w2[:].bitcast(I32), w2_words[:, 0].bitcast(I32).rearrange("e p b -> p e b"))
-        load_scales(s1, w1_scales, 2, E)
-        load_scales(s3, w3_scales, 2, E)
         load_words(1)
+        make_identity(nc, ident[:])
+        zero_plane(nc.gpsimd, s2)
+        load_scales(nc.sync, s3[1], w3_scales, 2, E)
+        nc.sync.dma_start(w2[:].bitcast(I32), w2_words[:, 0].bitcast(I32).rearrange("e p b -> p e b"))
+        load_scales(nc.sync, s2, w2_scales, 0, E)
         nc.sync.dma_start(gates[:], gate)
         load_words(2)
         load_words(3)
@@ -98,7 +105,7 @@ def tile_moe_res_glu_silu_kernel(tc, xT, xr, w1_words, w1_scales, w3_words, w3_s
 
         for c, (c0, n) in enumerate(CHUNKS):
             grouped = keep.tile([P, n, PACK], BF16, name="grouped%d" % c, align_bytes=64)
-            cut = n * 11 // 16
+            cut = n * 10 // 16
             src = raws[c][:].rearrange("p j w -> p w j")
             nc.vector.tensor_copy(grouped[:, 0:cut, :], src[:, 0:cut, :])
             nc.scalar.activation(grouped[:, cut:n, :], src[:, cut:n, :], COPY)
@@ -112,8 +119,8 @@ def tile_moe_res_glu_silu_kernel(tc, xT, xr, w1_words, w1_scales, w3_words, w3_s
 
         def gather(pair):
             where = offsets[:, pair * (PAIR // 16) : (pair + 1) * (PAIR // 16)]
-            codes = keep.tile([P, PAIR], U32, name="codes%d" % pair, align_bytes=64)
-            scales = keep.tile([P, PAIR], U8, name="scales%d" % pair, align_bytes=64)
+            codes = three.tile([P, PAIR], U32, name="codes", align_bytes=64)
+            scales = three.tile([P, PAIR], U8, name="scales", align_bytes=64)
             nc.vector.tensor_copy(codes[:], x_codes[:].indirect(where))
             nc.vector.tensor_copy(scales[:], x_scales[:].indirect(where))
             picked.append((codes, scales))
@@ -122,14 +129,15 @@ def tile_moe_res_glu_silu_kernel(tc, xT, xr, w1_words, w1_scales, w3_words, w3_s
             codes, scales = picked[e // 2]
             cols = slice(e % 2 * C, (e % 2 + 1) * C)
             sums = []
-            for held, plane, label in ((w1, s1, "a1"), (w3, s3, "a3")):
-                acc = psum.tile([P, H], F32, name=label)
+            planes = (s1[:, e, :], s3[0][:, e, :] if e < 2 else s3[1][:, e - 2, :])
+            for held, plane, label, pool in ((w1, planes[0], "a1", psum2), (w3, planes[1], "a3", psum3)):
+                acc = pool.tile([P, H], F32, name=label)
                 nc.tensor.matmul_mx(
                     out=acc[:],
                     lhsT=codes[:, cols].bitcast(FP8X4),
                     lhsT_scale=scales[:, cols],
                     rhs=held[e // 2][:, e % 2, :].bitcast(FP4X4),
-                    rhs_scale=plane[:, e, :],
+                    rhs_scale=plane,
                     start=True,
                     stop=True,
                 )
@@ -140,69 +148,78 @@ def tile_moe_res_glu_silu_kernel(tc, xT, xr, w1_words, w1_scales, w3_words, w3_s
 
         def product(a3, act):
             h = ring.tile([P, H], BF16, name="h", align_bytes=64)
-            nc.vector.tensor_tensor(h[:], a3[:], act[:], MULT)
-            turned = psum.tile([P, 2, C], F32, name="turned")
-            words = h[:].bitcast(F32)
-            for u in range(2):
-                nc.tensor.transpose(turned[:, u, :], words[:, u : H // 2 : 2], ident[:])
-            h_grouped = ring.tile([P, C * PACK], BF16, name="h_grouped", align_bytes=64)
+            halves = "p (q u d) -> p u q d"
+            nc.vector.tensor_tensor(
+                h[:].rearrange("p (u q d) -> p u q d", u=2, d=2),
+                a3[:].rearrange(halves, u=2, d=2),
+                act[:].rearrange(halves, u=2, d=2),
+                MULT,
+            )
+            return h
+
+        def turn(hs):
+            turned = psum2.tile([P, 2, 2, C], F32, name="turned")
+            for b in range(2):
+                words = hs[b][:].bitcast(F32)
+                for u in range(2):
+                    nc.tensor.transpose(turned[:, b, u, :], words[:, u * P : (u + 1) * P], ident[:])
+            h_grouped = two.tile([P, PAIR * PACK], BF16, name="h_grouped", align_bytes=64)
             nc.scalar.copy(
-                h_grouped[:].bitcast(F32).rearrange("p (r u) -> p r u", u=2),
-                turned[:].rearrange("p u r -> p r u"),
+                h_grouped[:].bitcast(F32).rearrange("p (b r u) -> p b r u", b=2, u=2),
+                turned[:].rearrange("p b u r -> p b r u"),
             )
             return h_grouped
 
-        def second(e, h_grouped, y):
-            h_codes = ring.tile([P, C], U32, name="h_codes", align_bytes=64)
-            h_scales = ring.tile([P, C], U8, name="h_scales", align_bytes=64)
+        def second(pair, h_grouped):
+            h_codes = two.tile([P, PAIR], U32, name="h_codes", align_bytes=64)
+            h_scales = two.tile([P, PAIR], U8, name="h_scales", align_bytes=64)
             nc.vector.quantize_mx(out=h_codes[:].bitcast(FP8X4), scales=h_scales[:], in_=h_grouped[:])
-            nc.tensor.matmul_mx(
-                out=y[:, e % 2, :],
-                lhsT=w2[:, e, :].bitcast(FP4X4),
-                lhsT_scale=s2[:, e, :],
-                rhs=h_codes[:].bitcast(FP8X4),
-                rhs_scale=h_scales[:],
-                start=True,
-                stop=True,
-            )
+            y = psum1.tile([P, PAIR], F32, name="y")
+            for b in range(2):
+                cols = slice(b * C, (b + 1) * C)
+                nc.tensor.matmul_mx(
+                    out=y[:, cols],
+                    lhsT=w2[:, 2 * pair + b, :].bitcast(FP4X4),
+                    lhsT_scale=s2[:, 2 * pair + b, :],
+                    rhs=h_codes[:, cols].bitcast(FP8X4),
+                    rhs_scale=h_scales[:, cols],
+                    start=True,
+                    stop=True,
+                )
+            return y
 
-        def scatter(pair, gated):
-            where = offsets[:, pair * (PAIR // 16) : (pair + 1) * (PAIR // 16)]
-            nc.vector.tensor_copy(back[:].indirect(where), gated[:])
-
-        sums = {}
         gated = {}
 
         def weigh(pair, y):
             tile = ring.tile([P, PAIR], F32, name="gated")
-            nc.vector.tensor_tensor(
-                tile[:], y[:].rearrange("p b c -> p (b c)"), gates[:, pair * PAIR : (pair + 1) * PAIR], MULT
-            )
+            nc.vector.tensor_tensor(tile[:], y[:], gates[:, pair * PAIR : (pair + 1) * PAIR], MULT)
             gated[pair] = tile
 
+        def scatter(pair):
+            where = offsets[:, pair * (PAIR // 16) : (pair + 1) * (PAIR // 16)]
+            nc.vector.tensor_copy(back[:].indirect(where), gated[pair][:])
+
         gather(0)
-        sums[0] = first(0)
-        sums[1] = first(1)
+        sums = {0: first(0), 1: first(1)}
         gather(1)
         y = None
         for pair in range(PAIRS):
-            grouped = []
+            hs = []
             for b in range(2):
-                grouped.append(product(*sums[2 * pair + b]))
+                hs.append(product(*sums[2 * pair + b]))
                 if pair + 1 < PAIRS:
                     sums[2 * pair + 2 + b] = first(2 * pair + 2 + b)
+            h_grouped = turn(hs)
             if pair >= 1:
                 weigh(pair - 1, y)
             if pair + 2 < PAIRS:
                 gather(pair + 2)
             if pair >= 2:
-                scatter(pair - 2, gated[pair - 2])
-            y = psum.tile([P, 2, C], F32, name="y")
-            for b in range(2):
-                second(2 * pair + b, grouped[b], y)
-        scatter(PAIRS - 2, gated[PAIRS - 2])
+                scatter(pair - 2)
+            y = second(pair, h_grouped)
+        scatter(PAIRS - 2)
         weigh(PAIRS - 1, y)
-        scatter(PAIRS - 1, gated[PAIRS - 1])
+        scatter(PAIRS - 1)
 
         for i, (c0, n) in enumerate(OUT_CUTS):
             done = keep.tile([P, n], F32, name="done%d" % i, align_bytes=64)

from contextlib import ExitStack

import concourse.mybir as mybir
from concourse.masks import make_identity

K, T, E, C, H, N = 512, 1536, 8, 128, 512, 128
S = E * C
FLOPS = 2 * S * (2 * K * H + H * N)

P = 128
PACK = 4
F32 = mybir.dt.float32
BF16 = mybir.dt.bfloat16
I32 = mybir.dt.int32
U32 = mybir.dt.uint32
U16 = mybir.dt.uint16
U8 = mybir.dt.uint8
FP8X4 = mybir.dt.float8_e4m3fn_x4
FP4X4 = mybir.dt.float4_e2m1fn_x4
MULT = mybir.AluOpType.mult
ADD = mybir.AluOpType.add
COPY = mybir.ActivationFunctionType.Copy
SILU = mybir.ActivationFunctionType.Silu

CHUNKS = ((0, 512), (512, 512), (1024, 256), (1280, 256))
PAIR = 2 * C
PAIRS = E // 2
OUT_CUTS = ((0, 640), (640, 512), (1152, 384))


def tile_moe_res_glu_silu_kernel(tc, xT, xr, w1_words, w1_scales, w3_words, w3_scales, w2_words, w2_scales, gate, offs, out):
    nc = tc.nc
    with ExitStack() as ctx:
        keep = ctx.enter_context(tc.tile_pool(name="keep", bufs=1))
        three = ctx.enter_context(tc.tile_pool(name="three", bufs=3))
        two = ctx.enter_context(tc.tile_pool(name="two", bufs=2))
        ring = ctx.enter_context(tc.tile_pool(name="ring", bufs=4))
        psum1 = ctx.enter_context(tc.psum_pool(name="psum1", bufs=1))
        psum2 = ctx.enter_context(tc.psum_pool(name="psum2", bufs=2))
        psum3 = ctx.enter_context(tc.psum_pool(name="psum3", bufs=3))

        offsets = keep.tile([P, S // 16], U16, name="offsets")
        ident = keep.tile([P, P], F32, name="ident", align_bytes=64)
        warm = keep.tile([P, 1], F32, name="warm")
        warm_out = keep.tile([P, 1], F32, name="warm_out")
        x_codes = keep.tile([P, T], U32, name="x_codes", align_bytes=64)
        x_scales = keep.tile([P, T], U8, name="x_scales", align_bytes=64)
        s1 = keep.tile([P, E, H], U8, name="s1", align_bytes=64)
        s3 = [keep.tile([P, n, H], U8, name="s3_%d" % n, align_bytes=64) for n in (2, E - 2)]
        s2 = keep.tile([P, E, N], U8, name="s2", align_bytes=64)
        w2 = keep.tile([P, E, 2 * N], U8, name="w2", align_bytes=64)
        gates = keep.tile([P, S], F32, name="gates", align_bytes=64)
        resid = keep.tile([P, T], F32, name="resid", align_bytes=64)
        back = keep.tile([P, T], F32, name="back", align_bytes=64)

        def zero_plane(engine, plane):
            engine.memset(plane[:].rearrange("p e i -> p (e i)").bitcast(I32), 0)

        zero_plane(nc.vector, s3[0])
        nc.vector.memset(warm[:], 0.0)
        nc.scalar.activation(warm_out[:], warm[:], SILU)
        zero_plane(nc.vector, s1)
        zero_plane(nc.vector, s3[1])
        nc.vector.memset(back[:], 0.0)
        nc.gpsimd.memset(x_scales[:].bitcast(I32), 0)

        raws = []
        for c, (c0, n) in enumerate(CHUNKS):
            raw = keep.tile([P, PACK, n], F32, name="raw%d" % c, align_bytes=64)
            nc.sync.dma_start(raw[:], xT[:, c0 : c0 + n].rearrange("(p j) w -> p j w", j=PACK))
            raws.append(raw)
        nc.sync.dma_start(offsets[:], offs)

        def load_scales(queue, tile, scales, e0, e1):
            for q in range(4):
                queue.dma_start(
                    tile[32 * q : 32 * q + 4].bitcast(I32),
                    scales[e0:e1, 0, 4 * q : 4 * q + 4, :].bitcast(I32).rearrange("e q i -> q e i"),
                )

        w1, w3 = [], []

        def load_words(pair):
            for held, words, label in ((w1, w1_words, "w1"), (w3, w3_words, "w3")):
                tile = keep.tile([P, 2, 2 * H], U8, name="%s_%d" % (label, pair), align_bytes=64)
                nc.sync.dma_start(
                    tile[:].bitcast(I32),
                    words[2 * pair : 2 * pair + 2, 0].bitcast(I32).rearrange("e p b -> p e b"),
                )
                held.append(tile)

        load_scales(nc.sync, s1, w1_scales, 0, E)
        load_scales(nc.gpsimd, s3[0], w3_scales, 0, 2)
        load_words(0)
        load_words(1)
        make_identity(nc, ident[:])
        zero_plane(nc.gpsimd, s2)
        load_scales(nc.sync, s3[1], w3_scales, 2, E)
        nc.sync.dma_start(w2[:].bitcast(I32), w2_words[:, 0].bitcast(I32).rearrange("e p b -> p e b"))
        load_scales(nc.sync, s2, w2_scales, 0, E)
        nc.sync.dma_start(gates[:], gate)
        load_words(2)
        load_words(3)
        nc.sync.dma_start(resid[:], xr)

        for c, (c0, n) in enumerate(CHUNKS):
            grouped = keep.tile([P, n, PACK], BF16, name="grouped%d" % c, align_bytes=64)
            cut = n * 10 // 16
            src = raws[c][:].rearrange("p j w -> p w j")
            nc.vector.tensor_copy(grouped[:, 0:cut, :], src[:, 0:cut, :])
            nc.scalar.activation(grouped[:, cut:n, :], src[:, cut:n, :], COPY)
            nc.vector.quantize_mx(
                out=x_codes[:, c0 : c0 + n].bitcast(FP8X4),
                scales=x_scales[:, c0 : c0 + n],
                in_=grouped[:].rearrange("p w j -> p (w j)"),
            )

        picked = []

        def gather(pair):
            where = offsets[:, pair * (PAIR // 16) : (pair + 1) * (PAIR // 16)]
            codes = three.tile([P, PAIR], U32, name="codes", align_bytes=64)
            scales = three.tile([P, PAIR], U8, name="scales", align_bytes=64)
            nc.vector.tensor_copy(codes[:], x_codes[:].indirect(where))
            nc.vector.tensor_copy(scales[:], x_scales[:].indirect(where))
            picked.append((codes, scales))

        def first(e):
            codes, scales = picked[e // 2]
            cols = slice(e % 2 * C, (e % 2 + 1) * C)
            sums = []
            planes = (s1[:, e, :], s3[0][:, e, :] if e < 2 else s3[1][:, e - 2, :])
            for held, plane, label, pool in ((w1, planes[0], "a1", psum2), (w3, planes[1], "a3", psum3)):
                acc = pool.tile([P, H], F32, name=label)
                nc.tensor.matmul_mx(
                    out=acc[:],
                    lhsT=codes[:, cols].bitcast(FP8X4),
                    lhsT_scale=scales[:, cols],
                    rhs=held[e // 2][:, e % 2, :].bitcast(FP4X4),
                    rhs_scale=plane,
                    start=True,
                    stop=True,
                )
                sums.append(acc)
            act = ring.tile([P, H], F32, name="act")
            nc.scalar.activation(act[:], sums[0][:], SILU)
            return sums[1], act

        def product(a3, act):
            h = ring.tile([P, H], BF16, name="h", align_bytes=64)
            halves = "p (q u d) -> p u q d"
            nc.vector.tensor_tensor(
                h[:].rearrange("p (u q d) -> p u q d", u=2, d=2),
                a3[:].rearrange(halves, u=2, d=2),
                act[:].rearrange(halves, u=2, d=2),
                MULT,
            )
            return h

        def turn(hs):
            turned = psum2.tile([P, 2, 2, C], F32, name="turned")
            for b in range(2):
                words = hs[b][:].bitcast(F32)
                for u in range(2):
                    nc.tensor.transpose(turned[:, b, u, :], words[:, u * P : (u + 1) * P], ident[:])
            h_grouped = two.tile([P, PAIR * PACK], BF16, name="h_grouped", align_bytes=64)
            nc.scalar.copy(
                h_grouped[:].bitcast(F32).rearrange("p (b r u) -> p b r u", b=2, u=2),
                turned[:].rearrange("p b u r -> p b r u"),
            )
            return h_grouped

        def second(pair, h_grouped):
            h_codes = two.tile([P, PAIR], U32, name="h_codes", align_bytes=64)
            h_scales = two.tile([P, PAIR], U8, name="h_scales", align_bytes=64)
            nc.vector.quantize_mx(out=h_codes[:].bitcast(FP8X4), scales=h_scales[:], in_=h_grouped[:])
            y = psum1.tile([P, PAIR], F32, name="y")
            for b in range(2):
                cols = slice(b * C, (b + 1) * C)
                nc.tensor.matmul_mx(
                    out=y[:, cols],
                    lhsT=w2[:, 2 * pair + b, :].bitcast(FP4X4),
                    lhsT_scale=s2[:, 2 * pair + b, :],
                    rhs=h_codes[:, cols].bitcast(FP8X4),
                    rhs_scale=h_scales[:, cols],
                    start=True,
                    stop=True,
                )
            return y

        gated = {}

        def weigh(pair, y):
            tile = ring.tile([P, PAIR], F32, name="gated")
            nc.vector.tensor_tensor(tile[:], y[:], gates[:, pair * PAIR : (pair + 1) * PAIR], MULT)
            gated[pair] = tile

        def scatter(pair):
            where = offsets[:, pair * (PAIR // 16) : (pair + 1) * (PAIR // 16)]
            nc.vector.tensor_copy(back[:].indirect(where), gated[pair][:])

        gather(0)
        sums = {0: first(0), 1: first(1)}
        gather(1)
        y = None
        for pair in range(PAIRS):
            hs = []
            for b in range(2):
                hs.append(product(*sums[2 * pair + b]))
                if pair + 1 < PAIRS:
                    sums[2 * pair + 2 + b] = first(2 * pair + 2 + b)
            h_grouped = turn(hs)
            if pair >= 1:
                weigh(pair - 1, y)
            if pair + 2 < PAIRS:
                gather(pair + 2)
            if pair >= 2:
                scatter(pair - 2)
            y = second(pair, h_grouped)
        scatter(PAIRS - 2)
        weigh(PAIRS - 1, y)
        scatter(PAIRS - 1)

        for i, (c0, n) in enumerate(OUT_CUTS):
            done = keep.tile([P, n], F32, name="done%d" % i, align_bytes=64)
            nc.vector.tensor_tensor(done[:], back[:, c0 : c0 + n], resid[:, c0 : c0 + n], ADD)
            nc.sync.dma_start(out[:, c0 : c0 + n], done[:])
